import numpy as np
import ml_dtypes


def mxq(x, axis, fmt="e4m3"):
    dtype, down = {"e4m3": (ml_dtypes.float8_e4m3fn, 7), "e5m2": (ml_dtypes.float8_e5m2, 14)}[fmt]
    v = np.moveaxis(np.asarray(x, np.float32).astype(ml_dtypes.bfloat16).astype(np.float64), axis, -1)
    blocks = v.reshape(v.shape[:-1] + (-1, 32))
    amax = np.abs(blocks).max(-1, keepdims=True)
    byte = np.maximum(np.where(amax > 0, np.frexp(amax)[1] - 1 + 127, 0) - down, 1)
    scale = np.exp2(byte - 127.0)
    codes = (blocks / scale).astype(np.float32).astype(dtype).astype(np.float64)
    return np.moveaxis((codes * scale).reshape(v.shape), -1, axis)


WIDE = False


def mx_kscale(k):
    if not WIDE:
        return np.ones(k)
    levels = np.array([10, -10, 5, -5, 0])
    if k % 512:
        return np.exp2(np.random.permutation(np.resize(levels, k // 32))).repeat(32)
    a = np.empty((k // 512, 16))
    for p in range(k // 512):
        a[p, :8] = np.random.permutation(np.resize(levels, 8))
        for g in range(8):
            far = levels[np.abs(levels - a[p, g]) >= 10]
            a[p, g + 8] = far[np.random.randint(len(far))]
    return np.exp2(a.ravel()).repeat(32)


def f64(x):
    return np.asarray(x).astype(np.float64)


def striped(idx):
    return np.tile(idx.reshape(-1, 16).T, (8, 1)).astype(np.uint16)


def unstriped(offs):
    return offs[:16].T.reshape(-1).astype(np.int64)


def pack_weight(w):
    k, n = w.shape
    w = f64(np.asarray(w, np.float32).astype(ml_dtypes.bfloat16)).reshape(k // 32, 32, n)
    amax = np.abs(w).max(1)
    byte = np.clip(np.where(amax > 0, np.frexp(amax)[1] - 1 + 127 - 7, 1), 1, 254)
    scaled = (w * np.exp2(127.0 - byte)[:, None, :]).reshape(k, n).astype(np.float32)
    words = np.ascontiguousarray(scaled.reshape(k // 512, 128, 4, n).transpose(0, 1, 3, 2)).astype(ml_dtypes.float8_e4m3fn).view(np.uint8)
    return words, np.ascontiguousarray(byte.astype(np.uint8).reshape(k // 512, 16, n))


def unpack_weight(words, scales):
    g, p, n, _ = words.shape
    vals = np.ascontiguousarray(words).view(ml_dtypes.float8_e4m3fn).astype(np.float64) * np.repeat(np.exp2(scales.astype(np.float64) - 127.0), 8, axis=1)[..., None]
    return vals.transpose(0, 1, 3, 2).reshape(g * 512, n)


def relu(v):
    return np.maximum(v, 0.0)


K, T, H, N = 512, 1024, 512, 256


def setup_inputs():
    n = np.random.standard_normal
    s = mx_kscale(K)[:, None]
    u = mx_kscale(H)
    packed_xT = pack_weight(n((K, T)) * s)
    return {
        "x_words": packed_xT[0],
        "x_scales": packed_xT[1],
        "w1": (n((K, H)) / np.sqrt(2 * K) / s * u).astype(np.float32),
        "w2": (n((K, H)) / np.sqrt(2 * K) / s * u).astype(np.float32),
        "w3": (n((H, N)) / np.sqrt(H) / u[:, None]).astype(np.float32),
        "pos1": striped(np.random.permutation(T)),
        "pos2": striped(np.random.permutation(T)),
    }


def reference(x_words, x_scales, w1, w2, w3, pos1, pos2):
    xq = unpack_weight(x_words, x_scales)
    y = mxq(f64(w1), 0, "e4m3").T @ xq
    e = mxq(f64(w2), 0, "e4m3").T @ xq
    z = np.maximum(relu(y + e[:, unstriped(pos1)]), relu(y + e[:, unstriped(pos2)]))
    return mxq(f64(w3), 0, "e4m3").T @ mxq(z, 0, "e4m3")

@@ -1,0 +1,227 @@
+from contextlib import ExitStack
+
+import concourse.mybir as mybir
+
+K, T, H, N = 512, 1024, 512, 256
+FLOPS = 2 * K * H * T * 2 + 2 * H * N * T
+
+F32 = mybir.dt.float32
+BF16 = mybir.dt.bfloat16
+I32 = mybir.dt.int32
+U32 = mybir.dt.uint32
+U16 = mybir.dt.uint16
+U8 = mybir.dt.uint8
+FP8X4 = mybir.dt.float8_e4m3fn_x4
+ADD = mybir.AluOpType.add
+MAX = mybir.AluOpType.max
+RELU = mybir.ActivationFunctionType.Relu
+
+P = 128
+PACK = 4
+BANK = 512
+HALF_H = H // 2
+CHUNKS = ((0, 512), (512, 256), (768, 128), (896, 128))
+
+
+def tile_picked_wedgecv_relu_l_kernel(
+    tc, x_words, x_scales, w1, w2, w3, pos1, pos2, out
+):
+    nc = tc.nc
+    with ExitStack() as ctx:
+        keep = ctx.enter_context(tc.tile_pool(name="keep", bufs=1))
+        ring = ctx.enter_context(tc.tile_pool(name="ring", bufs=2))
+        e_psum = ctx.enter_context(tc.psum_pool(name="e_psum", bufs=2))
+        y_psum = ctx.enter_context(tc.psum_pool(name="y_psum", bufs=4))
+        o_psum = ctx.enter_context(tc.psum_pool(name="o_psum", bufs=2))
+
+        list1 = keep.tile([P, T // 16], U16, name="list1")
+        list2 = keep.tile([P, T // 16], U16, name="list2")
+
+        x_plane = keep.tile([P, T], U8, name="x_plane", align_bytes=64)
+        nc.vector.memset(x_plane[:].bitcast(U32), 0)
+        for q in range(4):
+            nc.scalar.dma_start(
+                out=x_plane[32 * q : 32 * q + 4, :].bitcast(I32),
+                in_=x_scales[0, 4 * q : 4 * q + 4, :].bitcast(I32),
+            )
+
+        def load_halves(w, name):
+            halves = []
+            for h in range(2):
+                raw = keep.tile([P, PACK, HALF_H], F32, name=f"{name}_raw{h}")
+                cols = slice(h * HALF_H, (h + 1) * HALF_H)
+                nc.sync.dma_start(out=raw[:], in_=w[:, cols].rearrange("(p j) c -> p j c", j=PACK))
+                halves.append(raw)
+            return halves
+
+        w2_raw = load_halves(w2, "w2")
+        x_bytes = x_words[0].rearrange("p n r -> p (n r)")
+        x_codes = []
+        for h in range(2):
+            codes = keep.tile([P, BANK], U32, name=f"x_codes{h}", align_bytes=64)
+            nc.sync.dma_start(
+                out=codes[:].bitcast(I32),
+                in_=x_bytes[:, h * BANK * PACK : (h + 1) * BANK * PACK].bitcast(I32),
+            )
+            x_codes.append(codes)
+        nc.sync.dma_start(list1[:], pos1)
+        nc.sync.dma_start(list2[:], pos2)
+        w1_raw = load_halves(w1, "w1")
+        w3_raw = keep.tile([P, PACK, N], F32, name="w3_raw")
+        nc.sync.dma_start(out=w3_raw[:], in_=w3.rearrange("(p j) c -> p j c", j=PACK))
+
+        def deal_columns(copy, raw_halves, grouped):
+            for h, raw in enumerate(raw_halves):
+                m_half = slice(h * HALF_H // PACK, (h + 1) * HALF_H // PACK)
+                copy(
+                    out=grouped[:, :, m_half, :].rearrange("p t m j -> p m j t"),
+                    in_=raw[:].rearrange("p j (m t) -> p m j t", t=PACK),
+                )
+
+        def quantize(codes, scales, values):
+            nc.vector.quantize_mx(out=codes.bitcast(FP8X4), scales=scales, in_=values)
+
+        def project(acc, w_codes, w_scales, t, start, width):
+            h, lo = divmod(start, BANK)
+            rows = slice(t * P, (t + 1) * P)
+            nc.tensor.matmul_mx(
+                out=acc,
+                lhsT=w_codes[:, rows].bitcast(FP8X4),
+                lhsT_scale=w_scales[:, rows],
+                rhs=x_codes[h][:, lo : lo + width].bitcast(FP8X4),
+                rhs_scale=x_plane[:, start : start + width],
+                start=True,
+                stop=True,
+            )
+
+        w2_grouped = keep.tile([P, PACK, P, PACK], BF16, name="w2_grouped", align_bytes=64)
+        w2_codes = keep.tile([P, H], U32, name="w2_codes", align_bytes=64)
+        w2_scales = keep.tile([P, H], U8, name="w2_scales", align_bytes=64)
+        deal_columns(nc.vector.tensor_copy, w2_raw, w2_grouped)
+        w2_flat = w2_grouped[:].rearrange("p t m j -> p (t m j)")
+        for lo, hi in ((0, 128), (128, 256), (256, 512)):
+            quantize(w2_codes[:, lo:hi], w2_scales[:, lo:hi], w2_flat[:, lo * PACK : hi * PACK])
+
+        e_rows = [keep.tile([P, T], F32, name=f"e_rows{t}") for t in range(PACK)]
+
+        def make_e(t, copies):
+            for h in range(2):
+                acc = e_psum.tile([P, BANK], F32, name="e_acc")
+                project(acc[:], w2_codes, w2_scales, t, h * BANK, BANK)
+                copies[h](out=e_rows[t][:, h * BANK : (h + 1) * BANK], in_=acc[:])
+
+        def entries(lst, start, width):
+            return lst[:, start // 16 : (start + width) // 16]
+
+        make_e(0, (nc.scalar.copy, nc.vector.tensor_copy))
+
+        z_pre = keep.tile([P, PACK, T], F32, name="z_pre")
+        larger = keep.tile([P, T], F32, name="larger")
+
+        def gather_copy(t, lst, h, dst):
+            nc.vector.tensor_copy(dst[:], e_rows[t][:].indirect(entries(lst, h * BANK, BANK)))
+
+        g1a = keep.tile([P, BANK], F32, name="g1a")
+        g2a = keep.tile([P, BANK], F32, name="g2a")
+        g1b = keep.tile([P, BANK], F32, name="g1b")
+        gather_copy(0, list1, 0, g1a)
+        gather_copy(0, list2, 0, g2a)
+        gather_copy(0, list1, 1, g1b)
+        nc.vector.tensor_tensor(larger[:, :BANK], g1a[:], g2a[:], MAX)
+
+        make_e(1, (nc.scalar.copy, nc.scalar.copy))
+
+        w1_grouped = keep.tile([P, PACK, P, PACK], BF16, name="w1_grouped", tag="shared", align_bytes=64)
+        w1_codes = keep.tile([P, H], U32, name="w1_codes", align_bytes=64)
+        w1_scales = keep.tile([P, H], U8, name="w1_scales", align_bytes=64)
+        deal_columns(nc.scalar.copy, w1_raw, w1_grouped)
+        quantize(w1_codes[:], w1_scales[:], w1_grouped[:].rearrange("p t m j -> p (t m j)"))
+        g2b = keep.tile([P, BANK], F32, name="g2b", tag="shared", align_bytes=64)
+        gather_copy(0, list2, 1, g2b)
+        nc.vector.tensor_tensor(larger[:, BANK:], g1b[:], g2b[:], MAX)
+
+        y_rows = {}
+
+        def make_y(c, t):
+            start, width = CHUNKS[c]
+            acc = y_psum.tile([P, BANK], F32, name="y_acc")
+            project(acc[:, :width], w1_codes, w1_scales, t, start, width)
+            y_rows[c, t] = keep.tile([P, width], F32, name=f"y_rows{c}_{t}")
+            nc.scalar.copy(out=y_rows[c, t][:], in_=acc[:, :width])
+
+        def edges(c, t):
+            start, width = CHUNKS[c]
+            a = ring.tile([P, BANK], F32, name="edge1")
+            b = ring.tile([P, BANK], F32, name="edge2")
+            nc.vector.tensor_tensor(a[:, :width], e_rows[t][:].indirect(entries(list1, start, width)), y_rows[c, t][:], ADD)
+            nc.vector.tensor_tensor(b[:, :width], e_rows[t][:].indirect(entries(list2, start, width)), y_rows[c, t][:], ADD)
+            return a, b
+
+        def larger_edge(c, t, pair):
+            start, width = CHUNKS[c]
+            nc.vector.tensor_tensor(z_pre[:, t, start : start + width], pair[0][:, :width], pair[1][:, :width], MAX)
+
+        make_y(0, 1)
+        for h in range(2):
+            acc = y_psum.tile([P, BANK], F32, name="y_acc")
+            project(acc[:], w1_codes, w1_scales, 0, h * BANK, BANK)
+            cols = slice(h * BANK, (h + 1) * BANK)
+            nc.vector.tensor_tensor(z_pre[:, 0, cols], larger[:, cols], acc[:], ADD)
+        for t in (2, 3):
+            make_e(t, (nc.scalar.copy, nc.scalar.copy))
+            make_y(0, t)
+
+        w3_grouped = keep.tile([P, N, PACK], BF16, name="w3_grouped", align_bytes=64)
+        w3_codes = keep.tile([P, N], U32, name="w3_codes", align_bytes=64)
+        w3_scales = keep.tile([P, N], U8, name="w3_scales", align_bytes=64)
+        nc.scalar.copy(
+            out=w3_grouped[:].rearrange("p (c i) j -> p c j i", i=4),
+            in_=w3_raw[:].rearrange("p j (c i) -> p c j i", i=4),
+        )
+
+        out_view = out.rearrange("(g p) v -> p g v", p=P)
+
+        def finish(c):
+            start, width = CHUNKS[c]
+            last = c == len(CHUNKS) - 1
+            z16 = keep.tile([P, width, PACK], BF16, name=f"z16_{c}", align_bytes=64)
+            nc.scalar.activation(
+                out=z16[:].rearrange("p (c i) t -> p c t i", i=4),
+                in_=z_pre[:, :, start : start + width].rearrange("p t (c i) -> p c t i", i=4),
+                func=RELU,
+            )
+            z_codes = keep.tile([P, width], U32, name=f"z_codes{c}", align_bytes=64)
+            z_scales = keep.tile([P, width], U8, name=f"z_scales{c}", align_bytes=64)
+            quantize(z_codes[:], z_scales[:], z16[:].rearrange("p v t -> p (v t)"))
+            result = keep.tile([P, N // P, width], F32, name=f"result{c}")
+            for g in range(N // P):
+                acc = o_psum.tile([P, BANK], F32, name="o_acc")
+                nc.tensor.matmul_mx(
+                    out=acc[:, :width],
+                    lhsT=w3_codes[:, g * P : (g + 1) * P].bitcast(FP8X4),
+                    lhsT_scale=w3_scales[:, g * P : (g + 1) * P],
+                    rhs=z_codes[:].bitcast(FP8X4),
+                    rhs_scale=z_scales[:],
+                    start=True,
+                    stop=True,
+                )
+                copy = nc.vector.tensor_copy if last and g == 1 else nc.scalar.copy
+                copy(out=result[:, g, :], in_=acc[:, :width])
+            nc.sync.dma_start(out=out_view[:, :, start : start + width], in_=result[:])
+
+        units = [(c, t) for c in range(len(CHUNKS)) for t in (1, 2, 3)]
+        pending = None
+        for c, t in units:
+            if t == 1 and c + 1 < len(CHUNKS):
+                for u in (1, 2, 3):
+                    make_y(c + 1, u)
+            pair = edges(c, t)
+            if pending is not None:
+                larger_edge(*pending)
+                if pending[1] == 3:
+                    finish(pending[0])
+            pending = (c, t, pair)
+            if (c, t) == (0, 2):
+                quantize(w3_codes[:], w3_scales[:], w3_grouped[:].rearrange("p n j -> p (n j)"))
+        larger_edge(*pending)
+        finish(pending[0])

@@ -19,8 +19,10 @@ RELU = mybir.ActivationFunctionType.Relu
 P = 128
 PACK = 4
 BANK = 512
-HALF_H = H // 2
-CHUNKS = ((0, 512), (512, 256), (768, 128), (896, 128))
+W_PIECES = ((0, 320), (320, 192))
+MAIN = 896
+TAIL = T - MAIN
+PARTS = ((0, 512), (512, 384))
 
 
 def tile_picked_wedgecv_relu_l_kernel(
@@ -29,10 +31,10 @@ def tile_picked_wedgecv_relu_l_kernel(
     nc = tc.nc
     with ExitStack() as ctx:
         keep = ctx.enter_context(tc.tile_pool(name="keep", bufs=1))
-        ring = ctx.enter_context(tc.tile_pool(name="ring", bufs=2))
-        e_psum = ctx.enter_context(tc.psum_pool(name="e_psum", bufs=2))
-        y_psum = ctx.enter_context(tc.psum_pool(name="y_psum", bufs=4))
-        o_psum = ctx.enter_context(tc.psum_pool(name="o_psum", bufs=2))
+        psum = ctx.enter_context(tc.psum_pool(name="psum", bufs=1))
+
+        def bank(b):
+            return psum.tile([P, BANK], F32, name=f"bank{b}")
 
         list1 = keep.tile([P, T // 16], U16, name="list1")
         list2 = keep.tile([P, T // 16], U16, name="list2")
@@ -40,19 +42,18 @@ def tile_picked_wedgecv_relu_l_kernel(
         x_plane = keep.tile([P, T], U8, name="x_plane", align_bytes=64)
         nc.vector.memset(x_plane[:].bitcast(U32), 0)
         for q in range(4):
-            nc.scalar.dma_start(
+            nc.sync.dma_start(
                 out=x_plane[32 * q : 32 * q + 4, :].bitcast(I32),
                 in_=x_scales[0, 4 * q : 4 * q + 4, :].bitcast(I32),
             )
 
         def load_halves(w, name):
-            halves = []
-            for h in range(2):
-                raw = keep.tile([P, PACK, HALF_H], F32, name=f"{name}_raw{h}")
-                cols = slice(h * HALF_H, (h + 1) * HALF_H)
-                nc.sync.dma_start(out=raw[:], in_=w[:, cols].rearrange("(p j) c -> p j c", j=PACK))
-                halves.append(raw)
-            return halves
+            pieces = []
+            for lo, width in W_PIECES:
+                raw = keep.tile([P, PACK, width], F32, name=f"{name}_raw{lo}", tag=f"{name}_raw{lo}", align_bytes=64)
+                nc.sync.dma_start(out=raw[:], in_=w[:, lo : lo + width].rearrange("(p j) c -> p j c", j=PACK))
+                pieces.append(raw)
+            return pieces
 
         w2_raw = load_halves(w2, "w2")
         x_bytes = x_words[0].rearrange("p n r -> p (n r)")
@@ -70,13 +71,15 @@ def tile_picked_wedgecv_relu_l_kernel(
         w3_raw = keep.tile([P, PACK, N], F32, name="w3_raw")
         nc.sync.dma_start(out=w3_raw[:], in_=w3.rearrange("(p j) c -> p j c", j=PACK))
 
-        def deal_columns(copy, raw_halves, grouped):
-            for h, raw in enumerate(raw_halves):
-                m_half = slice(h * HALF_H // PACK, (h + 1) * HALF_H // PACK)
-                copy(
-                    out=grouped[:, :, m_half, :].rearrange("p t m j -> p m j t"),
-                    in_=raw[:].rearrange("p j (m t) -> p m j t", t=PACK),
-                )
+        def deal_columns(shares, raw_halves, grouped):
+            for (lo, width), raw in zip(W_PIECES, raw_halves):
+                groups = width // PACK
+                for copy, first, end in shares:
+                    a, b = groups * first // 24 * 2, groups * end // 24 * 2
+                    copy(
+                        out=grouped[:, :, lo // PACK + a : lo // PACK + b, :].rearrange("p t m j -> p m j t"),
+                        in_=raw[:, :, a * PACK : b * PACK].rearrange("p j (m t) -> p m j t", t=PACK),
+                    )
 
         def quantize(codes, scales, values):
             nc.vector.quantize_mx(out=codes.bitcast(FP8X4), scales=scales, in_=values)
@@ -97,131 +100,164 @@ def tile_picked_wedgecv_relu_l_kernel(
         w2_grouped = keep.tile([P, PACK, P, PACK], BF16, name="w2_grouped", align_bytes=64)
         w2_codes = keep.tile([P, H], U32, name="w2_codes", align_bytes=64)
         w2_scales = keep.tile([P, H], U8, name="w2_scales", align_bytes=64)
-        deal_columns(nc.vector.tensor_copy, w2_raw, w2_grouped)
+        deal_columns(((nc.vector.tensor_copy, 0, 8), (nc.scalar.copy, 8, 12)), w2_raw, w2_grouped)
         w2_flat = w2_grouped[:].rearrange("p t m j -> p (t m j)")
         for lo, hi in ((0, 128), (128, 256), (256, 512)):
             quantize(w2_codes[:, lo:hi], w2_scales[:, lo:hi], w2_flat[:, lo * PACK : hi * PACK])
 
-        e_rows = [keep.tile([P, T], F32, name=f"e_rows{t}") for t in range(PACK)]
+        e_rows = {0: keep.tile([P, T], F32, name="e_rows0")}
 
-        def make_e(t, copies):
+        def make_e(t, tag):
+            e_rows[t] = keep.tile([P, T], F32, name=f"e_rows{t}", tag=tag, align_bytes=64)
             for h in range(2):
-                acc = e_psum.tile([P, BANK], F32, name="e_acc")
+                acc = bank(2 + h)
                 project(acc[:], w2_codes, w2_scales, t, h * BANK, BANK)
-                copies[h](out=e_rows[t][:, h * BANK : (h + 1) * BANK], in_=acc[:])
+                nc.scalar.copy(out=e_rows[t][:, h * BANK : (h + 1) * BANK], in_=acc[:])
 
         def entries(lst, start, width):
             return lst[:, start // 16 : (start + width) // 16]
 
-        make_e(0, (nc.scalar.copy, nc.vector.tensor_copy))
+        for q in range(4):
+            acc = bank(q)
+            project(acc[:, :256], w2_codes, w2_scales, 0, q * 256, 256)
+            copy = nc.vector.tensor_copy if q % 2 else nc.scalar.copy
+            copy(out=e_rows[0][:, q * 256 : (q + 1) * 256], in_=acc[:, :256])
 
-        z_pre = keep.tile([P, PACK, T], F32, name="z_pre")
-        larger = keep.tile([P, T], F32, name="larger")
+        lists = (list1, list2)
 
-        def gather_copy(t, lst, h, dst):
-            nc.vector.tensor_copy(dst[:], e_rows[t][:].indirect(entries(lst, h * BANK, BANK)))
+        def pick(d, start, width, name, tag):
+            picked = keep.tile([P, width], F32, name=name, tag=tag, align_bytes=64)
+            nc.vector.tensor_copy(picked[:], e_rows[0][:].indirect(entries(lists[d], start, width)))
+            return picked
 
-        g1a = keep.tile([P, BANK], F32, name="g1a")
-        g2a = keep.tile([P, BANK], F32, name="g2a")
-        g1b = keep.tile([P, BANK], F32, name="g1b")
-        gather_copy(0, list1, 0, g1a)
-        gather_copy(0, list2, 0, g2a)
-        gather_copy(0, list1, 1, g1b)
-        nc.vector.tensor_tensor(larger[:, :BANK], g1a[:], g2a[:], MAX)
-
-        make_e(1, (nc.scalar.copy, nc.scalar.copy))
+        pick1 = pick(0, 0, MAIN, "pick1", "pick1")
+        pick2a = pick(1, 0, 512, "pick2a", "before_w3")
 
         w1_grouped = keep.tile([P, PACK, P, PACK], BF16, name="w1_grouped", tag="shared", align_bytes=64)
         w1_codes = keep.tile([P, H], U32, name="w1_codes", align_bytes=64)
         w1_scales = keep.tile([P, H], U8, name="w1_scales", align_bytes=64)
-        deal_columns(nc.scalar.copy, w1_raw, w1_grouped)
+        deal_columns(((nc.scalar.copy, 0, 12),), w1_raw, w1_grouped)
+        make_e(1, "w1_raw320")
         quantize(w1_codes[:], w1_scales[:], w1_grouped[:].rearrange("p t m j -> p (t m j)"))
-        g2b = keep.tile([P, BANK], F32, name="g2b", tag="shared", align_bytes=64)
-        gather_copy(0, list2, 1, g2b)
-        nc.vector.tensor_tensor(larger[:, BANK:], g1b[:], g2b[:], MAX)
+        pick2b = pick(1, 512, 384, "pick2b", "shared")
 
-        y_rows = {}
+        def centre(acc, lo, t, start, width):
+            project(acc[:, lo : lo + width], w1_codes, w1_scales, t, start, width)
 
-        def make_y(c, t):
-            start, width = CHUNKS[c]
-            acc = y_psum.tile([P, BANK], F32, name="y_acc")
-            project(acc[:, :width], w1_codes, w1_scales, t, start, width)
-            y_rows[c, t] = keep.tile([P, width], F32, name=f"y_rows{c}_{t}")
-            nc.scalar.copy(out=y_rows[c, t][:], in_=acc[:, :width])
+        main_edge = [keep.tile([P, PACK, MAIN], F32, name=f"main_edge{d}") for d in range(2)]
+        y1 = keep.tile([P, MAIN], F32, name="y1", tag="y1", align_bytes=64)
+        y23 = keep.tile([P, 2, MAIN], F32, name="y23", tag="y23", align_bytes=64)
+        y_tail = keep.tile([P, PACK, TAIL], F32, name="y_tail")
 
-        def edges(c, t):
-            start, width = CHUNKS[c]
-            a = ring.tile([P, BANK], F32, name="edge1")
-            b = ring.tile([P, BANK], F32, name="edge2")
-            nc.vector.tensor_tensor(a[:, :width], e_rows[t][:].indirect(entries(list1, start, width)), y_rows[c, t][:], ADD)
-            nc.vector.tensor_tensor(b[:, :width], e_rows[t][:].indirect(entries(list2, start, width)), y_rows[c, t][:], ADD)
-            return a, b
+        y0a = bank(1)
+        centre(y0a, 0, 0, 0, 512)
+        acc = bank(0)
+        centre(acc, 0, 1, 0, 512)
+        nc.scalar.copy(out=y1[:, :512], in_=acc[:])
+        acc = bank(4)
+        centre(acc, 0, 1, 512, 256)
+        centre(acc, 256, 1, 768, 128)
+        nc.scalar.copy(out=y1[:, 512:], in_=acc[:, :384])
+        y0b = bank(5)
+        centre(y0b, 0, 0, 512, 256)
+        centre(y0b, 256, 0, 768, 128)
+        nc.vector.tensor_tensor(main_edge[0][:, 0, :512], pick1[:, :512], y0a[:], ADD)
+        nc.vector.tensor_tensor(main_edge[1][:, 0, :512], pick2a[:], y0a[:], ADD)
+        nc.vector.tensor_tensor(main_edge[0][:, 0, 512:], pick1[:, 512:], y0b[:, :384], ADD)
+        nc.vector.tensor_tensor(main_edge[1][:, 0, 512:], pick2b[:], y0b[:, :384], ADD)
 
-        def larger_edge(c, t, pair):
-            start, width = CHUNKS[c]
-            nc.vector.tensor_tensor(z_pre[:, t, start : start + width], pair[0][:, :width], pair[1][:, :width], MAX)
+        def edge(dst, d, t, start, width, y):
+            nc.vector.tensor_tensor(dst, e_rows[t][:].indirect(entries(lists[d], start, width)), y, ADD)
 
-        make_y(0, 1)
-        for h in range(2):
-            acc = y_psum.tile([P, BANK], F32, name="y_acc")
-            project(acc[:], w1_codes, w1_scales, 0, h * BANK, BANK)
-            cols = slice(h * BANK, (h + 1) * BANK)
-            nc.vector.tensor_tensor(z_pre[:, 0, cols], larger[:, cols], acc[:], ADD)
-        for t in (2, 3):
-            make_e(t, (nc.scalar.copy, nc.scalar.copy))
-            make_y(0, t)
+        for d in range(2):
+            edge(main_edge[d][:, 1, :], d, 1, 0, MAIN, y1[:])
 
-        w3_grouped = keep.tile([P, N, PACK], BF16, name="w3_grouped", align_bytes=64)
+        make_e(2, "e2")
+        make_e(3, "e3")
+        for i in range(2):
+            acc = bank(6 + i)
+            centre(acc, 0, 2 + i, 0, 512)
+            nc.scalar.copy(out=y23[:, i, :512], in_=acc[:])
+        for b, start, width in ((0, 768, 128), (4, 512, 256)):
+            acc = bank(b)
+            for i in range(2):
+                centre(acc, i * width, 2 + i, start, width)
+            nc.scalar.copy(
+                out=y23[:, :, start : start + width],
+                in_=acc[:, : 2 * width].rearrange("p (i v) -> p i v", i=2),
+            )
+
+        w3_grouped = keep.tile([P, N, PACK], BF16, name="w3_grouped", tag="before_w3", align_bytes=64)
         w3_codes = keep.tile([P, N], U32, name="w3_codes", align_bytes=64)
         w3_scales = keep.tile([P, N], U8, name="w3_scales", align_bytes=64)
         nc.scalar.copy(
             out=w3_grouped[:].rearrange("p (c i) j -> p c j i", i=4),
             in_=w3_raw[:].rearrange("p j (c i) -> p c j i", i=4),
         )
+        acc = bank(1)
+        for t in range(PACK):
+            centre(acc, t * TAIL, t, MAIN, TAIL)
+        nc.scalar.copy(out=y_tail[:].rearrange("p t v -> p (t v)"), in_=acc[:])
+
+        def woven(ap):
+            return ap.rearrange("p (c i) t -> p c t i", i=4)
+
+        def planar(ap):
+            return ap.rearrange("p t (c i) -> p c t i", i=4)
+
+        def round_edges(src, name):
+            rounded = keep.tile([P, src.shape[2], PACK], BF16, name=name, align_bytes=64)
+            nc.scalar.activation(out=woven(rounded[:]), in_=planar(src), func=RELU)
+            return rounded
+
+        rounded = {}
+        for t in (2, 3):
+            edge(main_edge[0][:, t, :], 0, t, 0, MAIN, y23[:, t - 2, :])
+        quantize(w3_codes[:], w3_scales[:], w3_grouped[:].rearrange("p n j -> p (n j)"))
+        for start, width in PARTS:
+            cols = slice(start, start + width)
+            for t in (2, 3):
+                edge(main_edge[1][:, t, cols], 1, t, start, width, y23[:, t - 2, cols])
+            for d in range(2):
+                rounded[d, start] = round_edges(main_edge[d][:, :, cols], f"rounded{d}_{start}")
 
         out_view = out.rearrange("(g p) v -> p g v", p=P)
 
-        def finish(c):
-            start, width = CHUNKS[c]
-            last = c == len(CHUNKS) - 1
-            z16 = keep.tile([P, width, PACK], BF16, name=f"z16_{c}", align_bytes=64)
-            nc.scalar.activation(
-                out=z16[:].rearrange("p (c i) t -> p c t i", i=4),
-                in_=z_pre[:, :, start : start + width].rearrange("p t (c i) -> p c t i", i=4),
-                func=RELU,
-            )
-            z_codes = keep.tile([P, width], U32, name=f"z_codes{c}", align_bytes=64)
-            z_scales = keep.tile([P, width], U8, name=f"z_scales{c}", align_bytes=64)
-            quantize(z_codes[:], z_scales[:], z16[:].rearrange("p v t -> p (v t)"))
-            result = keep.tile([P, N // P, width], F32, name=f"result{c}")
+        def finish(z16, start, pieces, banks, copies):
+            width = sum(pieces)
+            z_codes = keep.tile([P, width], U32, name=f"z_codes{start}", align_bytes=64)
+            z_scales = keep.tile([P, width], U8, name=f"z_scales{start}", align_bytes=64)
+            result = keep.tile([P, N // P, width], F32, name=f"result{start}")
+            accs = [bank(b) for b in banks]
+            lo = 0
+            for piece in pieces:
+                cols = slice(lo, lo + piece)
+                quantize(z_codes[:, cols], z_scales[:, cols], z16[:, cols, :].rearrange("p v t -> p (v t)"))
+                for g in range(N // P):
+                    nc.tensor.matmul_mx(
+                        out=accs[g][:, cols],
+                        lhsT=w3_codes[:, g * P : (g + 1) * P].bitcast(FP8X4),
+                        lhsT_scale=w3_scales[:, g * P : (g + 1) * P],
+                        rhs=z_codes[:, cols].bitcast(FP8X4),
+                        rhs_scale=z_scales[:, cols],
+                        start=True,
+                        stop=True,
+                    )
+                lo += piece
             for g in range(N // P):
-                acc = o_psum.tile([P, BANK], F32, name="o_acc")
-                nc.tensor.matmul_mx(
-                    out=acc[:, :width],
-                    lhsT=w3_codes[:, g * P : (g + 1) * P].bitcast(FP8X4),
-                    lhsT_scale=w3_scales[:, g * P : (g + 1) * P],
-                    rhs=z_codes[:].bitcast(FP8X4),
-                    rhs_scale=z_scales[:],
-                    start=True,
-                    stop=True,
-                )
-                copy = nc.vector.tensor_copy if last and g == 1 else nc.scalar.copy
-                copy(out=result[:, g, :], in_=acc[:, :width])
+                copies[g](out=result[:, g, :], in_=accs[g][:, :width])
             nc.sync.dma_start(out=out_view[:, :, start : start + width], in_=result[:])
 
-        units = [(c, t) for c in range(len(CHUNKS)) for t in (1, 2, 3)]
-        pending = None
-        for c, t in units:
-            if t == 1 and c + 1 < len(CHUNKS):
-                for u in (1, 2, 3):
-                    make_y(c + 1, u)
-            pair = edges(c, t)
-            if pending is not None:
-                larger_edge(*pending)
-                if pending[1] == 3:
-                    finish(pending[0])
-            pending = (c, t, pair)
-            if (c, t) == (0, 2):
-                quantize(w3_codes[:], w3_scales[:], w3_grouped[:].rearrange("p n j -> p (n j)"))
-        larger_edge(*pending)
-        finish(pending[0])
+        tail_edge = []
+        for d, (start, width), pieces, banks in zip(range(2), PARTS, ((512,), (256, 128)), ((6, 7), (2, 3))):
+            z16 = keep.tile([P, width, PACK], BF16, name=f"z16_{start}", tag=f"z{d}", align_bytes=64)
+            nc.vector.tensor_tensor(z16[:], rounded[0, start][:], rounded[1, start][:], MAX)
+            finish(z16, start, pieces, banks, (nc.scalar.copy, nc.scalar.copy))
+            tail_edge.append(keep.tile([P, PACK, TAIL], F32, name=f"tail_edge{d}", tag=f"z{d}", align_bytes=64))
+            for t in range(PACK):
+                edge(tail_edge[d][:, t, :], d, t, MAIN, TAIL, y_tail[:, t, :])
+            if d == 0:
+                tail_rounded = round_edges(tail_edge[0][:], "tail_rounded")
+        z16 = keep.tile([P, TAIL, PACK], BF16, name="z16_tail", align_bytes=64)
+        nc.vector.tensor_tensor(woven(z16[:]), woven(tail_rounded[:]), planar(tail_edge[1][:]), MAX)
+        finish(z16, MAIN, (TAIL,), (4, 5), (nc.scalar.copy, nc.vector.tensor_copy))

@@ -19,10 +19,15 @@ RELU = mybir.ActivationFunctionType.Relu
 P = 128
 PACK = 4
 BANK = 512
+STRIPE = 16
+RUN = 4
 W_PIECES = ((0, 320), (320, 192))
+E0_PIECES = ((0, 256), (256, 256), (512, 256), (768, 128), (896, 128))
+E0_BANKS = (0, 1, 2, 4, 3)
 MAIN = 896
 TAIL = T - MAIN
-PARTS = ((0, 512), (512, 384))
+PARTS = ((0, BANK), (BANK, MAIN - BANK))
+WIDE, NARROW = 256, 128
 
 
 def tile_picked_wedgecv_relu_l_kernel(
@@ -36,29 +41,31 @@ def tile_picked_wedgecv_relu_l_kernel(
         def bank(b):
             return psum.tile([P, BANK], F32, name=f"bank{b}")
 
-        list1 = keep.tile([P, T // 16], U16, name="list1")
-        list2 = keep.tile([P, T // 16], U16, name="list2")
+        list1 = keep.tile([P, T // STRIPE], U16, name="list1")
+        list2 = keep.tile([P, T // STRIPE], U16, name="list2")
 
-        x_plane = keep.tile([P, T], U8, name="x_plane", align_bytes=64)
-        nc.vector.memset(x_plane[:].bitcast(U32), 0)
+        x_scale_rows = keep.tile([P, T], U8, name="x_scale_rows", align_bytes=64)
+        nc.vector.memset(x_scale_rows[:].bitcast(U32), 0)
         for q in range(4):
             nc.sync.dma_start(
-                out=x_plane[32 * q : 32 * q + 4, :].bitcast(I32),
+                out=x_scale_rows[32 * q : 32 * q + 4, :].bitcast(I32),
                 in_=x_scales[0, 4 * q : 4 * q + 4, :].bitcast(I32),
             )
 
-        def load_halves(w, name):
+        def load_pieces(w, name):
             pieces = []
-            for lo, width in W_PIECES:
-                raw = keep.tile([P, PACK, width], F32, name=f"{name}_raw{lo}", tag=f"{name}_raw{lo}", align_bytes=64)
-                nc.sync.dma_start(out=raw[:], in_=w[:, lo : lo + width].rearrange("(p j) c -> p j c", j=PACK))
+            for first, width in W_PIECES:
+                raw = keep.tile(
+                    [P, PACK, width], F32, name=f"{name}_raw{first}", tag=f"{name}_raw{first}", align_bytes=64
+                )
+                nc.sync.dma_start(out=raw[:], in_=w[:, first : first + width].rearrange("(p j) c -> p j c", j=PACK))
                 pieces.append(raw)
             return pieces
 
-        w2_raw = load_halves(w2, "w2")
+        w2_raw = load_pieces(w2, "w2")
         x_bytes = x_words[0].rearrange("p n r -> p (n r)")
         x_codes = []
-        for h in range(2):
+        for h in range(T // BANK):
             codes = keep.tile([P, BANK], U32, name=f"x_codes{h}", align_bytes=64)
             nc.sync.dma_start(
                 out=codes[:].bitcast(I32),
@@ -67,19 +74,16 @@ def tile_picked_wedgecv_relu_l_kernel(
             x_codes.append(codes)
         nc.sync.dma_start(list1[:], pos1)
         nc.sync.dma_start(list2[:], pos2)
-        w1_raw = load_halves(w1, "w1")
+        w1_raw = load_pieces(w1, "w1")
         w3_raw = keep.tile([P, PACK, N], F32, name="w3_raw")
         nc.sync.dma_start(out=w3_raw[:], in_=w3.rearrange("(p j) c -> p j c", j=PACK))
 
-        def deal_columns(shares, raw_halves, grouped):
-            for (lo, width), raw in zip(W_PIECES, raw_halves):
-                groups = width // PACK
-                for copy, first, end in shares:
-                    a, b = groups * first // 24 * 2, groups * end // 24 * 2
-                    copy(
-                        out=grouped[:, :, lo // PACK + a : lo // PACK + b, :].rearrange("p t m j -> p m j t"),
-                        in_=raw[:, :, a * PACK : b * PACK].rearrange("p j (m t) -> p m j t", t=PACK),
-                    )
+        def deal_columns(copy, raw, first, m_lo, m_hi, grouped):
+            m0 = first // PACK
+            copy(
+                out=grouped[:, :, m0 + m_lo : m0 + m_hi, :].rearrange("p t m j -> p m j t"),
+                in_=raw[:, :, m_lo * PACK : m_hi * PACK].rearrange("p j (m t) -> p m j t", t=PACK),
+            )
 
         def quantize(codes, scales, values):
             nc.vector.quantize_mx(out=codes.bitcast(FP8X4), scales=scales, in_=values)
@@ -92,7 +96,7 @@ def tile_picked_wedgecv_relu_l_kernel(
                 lhsT=w_codes[:, rows].bitcast(FP8X4),
                 lhsT_scale=w_scales[:, rows],
                 rhs=x_codes[h][:, lo : lo + width].bitcast(FP8X4),
-                rhs_scale=x_plane[:, start : start + width],
+                rhs_scale=x_scale_rows[:, start : start + width],
                 start=True,
                 stop=True,
             )
@@ -100,85 +104,92 @@ def tile_picked_wedgecv_relu_l_kernel(
         w2_grouped = keep.tile([P, PACK, P, PACK], BF16, name="w2_grouped", align_bytes=64)
         w2_codes = keep.tile([P, H], U32, name="w2_codes", align_bytes=64)
         w2_scales = keep.tile([P, H], U8, name="w2_scales", align_bytes=64)
-        deal_columns(((nc.vector.tensor_copy, 0, 8), (nc.scalar.copy, 8, 12)), w2_raw, w2_grouped)
+        for (first, width), raw in zip(W_PIECES, w2_raw):
+            groups = width // PACK
+            vector_groups = groups // 3 * 2
+            deal_columns(nc.vector.tensor_copy, raw, first, 0, vector_groups, w2_grouped)
+            deal_columns(nc.scalar.copy, raw, first, vector_groups, groups, w2_grouped)
         w2_flat = w2_grouped[:].rearrange("p t m j -> p (t m j)")
-        for lo, hi in ((0, 128), (128, 256), (256, 512)):
+        for lo, hi in ((0, P), (P, 2 * P), (2 * P, H)):
             quantize(w2_codes[:, lo:hi], w2_scales[:, lo:hi], w2_flat[:, lo * PACK : hi * PACK])
 
         e_rows = {0: keep.tile([P, T], F32, name="e_rows0")}
 
         def make_e(t, tag):
             e_rows[t] = keep.tile([P, T], F32, name=f"e_rows{t}", tag=tag, align_bytes=64)
-            for h in range(2):
+            for h in range(T // BANK):
                 acc = bank(2 + h)
                 project(acc[:], w2_codes, w2_scales, t, h * BANK, BANK)
                 nc.scalar.copy(out=e_rows[t][:, h * BANK : (h + 1) * BANK], in_=acc[:])
 
-        def entries(lst, start, width):
-            return lst[:, start // 16 : (start + width) // 16]
-
-        for q in range(4):
-            acc = bank(q)
-            project(acc[:, :256], w2_codes, w2_scales, 0, q * 256, 256)
+        for q, (start, width) in enumerate(E0_PIECES):
+            acc = bank(E0_BANKS[q])
+            project(acc[:, :width], w2_codes, w2_scales, 0, start, width)
             copy = nc.vector.tensor_copy if q % 2 else nc.scalar.copy
-            copy(out=e_rows[0][:, q * 256 : (q + 1) * 256], in_=acc[:, :256])
+            copy(out=e_rows[0][:, start : start + width], in_=acc[:, :width])
 
         lists = (list1, list2)
 
+        def neighbours(d, t, start, width):
+            return e_rows[t][:].indirect(lists[d][:, start // STRIPE : (start + width) // STRIPE])
+
         def pick(d, start, width, name, tag):
             picked = keep.tile([P, width], F32, name=name, tag=tag, align_bytes=64)
-            nc.vector.tensor_copy(picked[:], e_rows[0][:].indirect(entries(lists[d], start, width)))
+            nc.vector.tensor_copy(picked[:], neighbours(d, 0, start, width))
             return picked
 
         pick1 = pick(0, 0, MAIN, "pick1", "pick1")
-        pick2a = pick(1, 0, 512, "pick2a", "before_w3")
+        pick2_low = pick(1, 0, BANK, "pick2_low", "pick2_low_then_w3")
 
-        w1_grouped = keep.tile([P, PACK, P, PACK], BF16, name="w1_grouped", tag="shared", align_bytes=64)
+        w1_grouped = keep.tile([P, PACK, P, PACK], BF16, name="w1_grouped", tag="w1_then_pick2_high", align_bytes=64)
         w1_codes = keep.tile([P, H], U32, name="w1_codes", align_bytes=64)
         w1_scales = keep.tile([P, H], U8, name="w1_scales", align_bytes=64)
-        deal_columns(((nc.scalar.copy, 0, 12),), w1_raw, w1_grouped)
-        make_e(1, "w1_raw320")
+        for (first, width), raw in zip(W_PIECES, w1_raw):
+            deal_columns(nc.scalar.copy, raw, first, 0, width // PACK, w1_grouped)
+        make_e(1, f"w1_raw{W_PIECES[-1][0]}")
         quantize(w1_codes[:], w1_scales[:], w1_grouped[:].rearrange("p t m j -> p (t m j)"))
-        pick2b = pick(1, 512, 384, "pick2b", "shared")
+        pick2_high = pick(1, BANK, MAIN - BANK, "pick2_high", "w1_then_pick2_high")
 
         def centre(acc, lo, t, start, width):
             project(acc[:, lo : lo + width], w1_codes, w1_scales, t, start, width)
 
-        main_edge = [keep.tile([P, PACK, MAIN], F32, name=f"main_edge{d}") for d in range(2)]
-        y1 = keep.tile([P, MAIN], F32, name="y1", tag="y1", align_bytes=64)
-        y23 = keep.tile([P, 2, MAIN], F32, name="y23", tag="y23", align_bytes=64)
+        mid_edges = [keep.tile([P, 2, MAIN], F32, name=f"mid_edges{d}") for d in range(2)]
+        z_planar = keep.tile([P, PACK, MAIN], BF16, name="z_planar")
+        larger_e0 = keep.tile([P, MAIN], F32, name="larger_e0")
+        nc.vector.tensor_tensor(larger_e0[:, :BANK], pick1[:, :BANK], pick2_low[:], MAX)
+        nc.vector.tensor_tensor(larger_e0[:, BANK:], pick1[:, BANK:], pick2_high[:], MAX)
+        y1 = keep.tile([P, MAIN], F32, name="y1", align_bytes=64)
+        y23 = keep.tile([P, 2, MAIN], F32, name="y23", align_bytes=64)
         y_tail = keep.tile([P, PACK, TAIL], F32, name="y_tail")
 
-        y0a = bank(1)
-        centre(y0a, 0, 0, 0, 512)
+        y0_low = bank(1)
+        centre(y0_low, 0, 0, 0, BANK)
         acc = bank(0)
-        centre(acc, 0, 1, 0, 512)
-        nc.scalar.copy(out=y1[:, :512], in_=acc[:])
+        centre(acc, 0, 1, 0, BANK)
+        nc.scalar.copy(out=y1[:, :BANK], in_=acc[:])
         acc = bank(4)
-        centre(acc, 0, 1, 512, 256)
-        centre(acc, 256, 1, 768, 128)
-        nc.scalar.copy(out=y1[:, 512:], in_=acc[:, :384])
-        y0b = bank(5)
-        centre(y0b, 0, 0, 512, 256)
-        centre(y0b, 256, 0, 768, 128)
-        nc.vector.tensor_tensor(main_edge[0][:, 0, :512], pick1[:, :512], y0a[:], ADD)
-        nc.vector.tensor_tensor(main_edge[1][:, 0, :512], pick2a[:], y0a[:], ADD)
-        nc.vector.tensor_tensor(main_edge[0][:, 0, 512:], pick1[:, 512:], y0b[:, :384], ADD)
-        nc.vector.tensor_tensor(main_edge[1][:, 0, 512:], pick2b[:], y0b[:, :384], ADD)
+        centre(acc, 0, 1, BANK, WIDE)
+        centre(acc, WIDE, 1, BANK + WIDE, NARROW)
+        nc.scalar.copy(out=y1[:, BANK:], in_=acc[:, : MAIN - BANK])
+        y0_high = bank(5)
+        centre(y0_high, 0, 0, BANK, WIDE)
+        centre(y0_high, WIDE, 0, BANK + WIDE, NARROW)
+        nc.vector.tensor_tensor(z_planar[:, 0, :BANK], larger_e0[:, :BANK], y0_low[:], ADD)
+        nc.vector.tensor_tensor(z_planar[:, 0, BANK:], larger_e0[:, BANK:], y0_high[:, : MAIN - BANK], ADD)
 
         def edge(dst, d, t, start, width, y):
-            nc.vector.tensor_tensor(dst, e_rows[t][:].indirect(entries(lists[d], start, width)), y, ADD)
+            nc.vector.tensor_tensor(dst, neighbours(d, t, start, width), y, ADD)
 
         for d in range(2):
-            edge(main_edge[d][:, 1, :], d, 1, 0, MAIN, y1[:])
+            edge(mid_edges[d][:, 0, :], d, 1, 0, MAIN, y1[:])
 
-        make_e(2, "e2")
-        make_e(3, "e3")
+        make_e(2, "e_rows2")
+        make_e(3, "e_rows3")
         for i in range(2):
             acc = bank(6 + i)
-            centre(acc, 0, 2 + i, 0, 512)
-            nc.scalar.copy(out=y23[:, i, :512], in_=acc[:])
-        for b, start, width in ((0, 768, 128), (4, 512, 256)):
+            centre(acc, 0, 2 + i, 0, BANK)
+            nc.scalar.copy(out=y23[:, i, :BANK], in_=acc[:])
+        for b, start, width in ((0, BANK + WIDE, NARROW), (4, BANK, WIDE)):
             acc = bank(b)
             for i in range(2):
                 centre(acc, i * width, 2 + i, start, width)
@@ -187,52 +198,62 @@ def tile_picked_wedgecv_relu_l_kernel(
                 in_=acc[:, : 2 * width].rearrange("p (i v) -> p i v", i=2),
             )
 
-        w3_grouped = keep.tile([P, N, PACK], BF16, name="w3_grouped", tag="before_w3", align_bytes=64)
+        w3_grouped = keep.tile([P, N, PACK], BF16, name="w3_grouped", tag="pick2_low_then_w3", align_bytes=64)
         w3_codes = keep.tile([P, N], U32, name="w3_codes", align_bytes=64)
         w3_scales = keep.tile([P, N], U8, name="w3_scales", align_bytes=64)
         nc.scalar.copy(
-            out=w3_grouped[:].rearrange("p (c i) j -> p c j i", i=4),
-            in_=w3_raw[:].rearrange("p j (c i) -> p c j i", i=4),
+            out=w3_grouped[:].rearrange("p (c i) j -> p c j i", i=RUN),
+            in_=w3_raw[:].rearrange("p j (c i) -> p c j i", i=RUN),
         )
-        acc = bank(1)
+        acc = bank(4)
         for t in range(PACK):
             centre(acc, t * TAIL, t, MAIN, TAIL)
         nc.scalar.copy(out=y_tail[:].rearrange("p t v -> p (t v)"), in_=acc[:])
 
         def woven(ap):
-            return ap.rearrange("p (c i) t -> p c t i", i=4)
+            return ap.rearrange("p (c i) t -> p c t i", i=RUN)
 
         def planar(ap):
-            return ap.rearrange("p t (c i) -> p c t i", i=4)
+            return ap.rearrange("p t (c i) -> p c t i", i=RUN)
 
-        def round_edges(src, name):
-            rounded = keep.tile([P, src.shape[2], PACK], BF16, name=name, align_bytes=64)
-            nc.scalar.activation(out=woven(rounded[:]), in_=planar(src), func=RELU)
-            return rounded
+        def relu_and_weave(src, name):
+            dst = keep.tile([P, src.shape[2], PACK], BF16, name=name, tag=name, align_bytes=64)
+            nc.scalar.activation(out=woven(dst[:]), in_=planar(src), func=RELU)
+            return dst
 
-        rounded = {}
-        for t in (2, 3):
-            edge(main_edge[0][:, t, :], 0, t, 0, MAIN, y23[:, t - 2, :])
+        for d in range(2):
+            edge(mid_edges[d][:, 1, :], d, 2, 0, MAIN, y23[:, 0, :])
         quantize(w3_codes[:], w3_scales[:], w3_grouped[:].rearrange("p n j -> p (n j)"))
-        for start, width in PARTS:
+        rounded = {}
+        for d in range(2):
+            for start, width in PARTS:
+                rounded[d, start] = keep.tile(
+                    [P, 2, width], BF16, name=f"rounded{d}_{start}", tag=f"rounded{d}_{start}", align_bytes=64
+                )
+                nc.scalar.copy(out=rounded[d, start][:], in_=mid_edges[d][:, :, start : start + width])
+        last_edge1 = keep.tile([P, MAIN], F32, name="last_edge1")
+        edge(last_edge1[:], 0, 3, 0, MAIN, y23[:, 1, :])
+        z_woven = []
+        for (start, width), tag in zip(PARTS, ("last_edge2_0", "rounded0_0")):
             cols = slice(start, start + width)
-            for t in (2, 3):
-                edge(main_edge[1][:, t, cols], 1, t, start, width, y23[:, t - 2, cols])
-            for d in range(2):
-                rounded[d, start] = round_edges(main_edge[d][:, :, cols], f"rounded{d}_{start}")
+            last_edge2 = keep.tile([P, width], F32, name=f"last_edge2_{start}", tag=tag, align_bytes=64)
+            edge(last_edge2[:], 1, 3, start, width, y23[:, 1, cols])
+            nc.vector.tensor_tensor(z_planar[:, 1:3, cols], rounded[0, start][:], rounded[1, start][:], MAX)
+            nc.vector.tensor_tensor(z_planar[:, 3, cols], last_edge1[:, cols], last_edge2[:], MAX)
+            z_woven.append(relu_and_weave(z_planar[:, :, cols], f"z_woven{start}"))
 
         out_view = out.rearrange("(g p) v -> p g v", p=P)
 
-        def finish(z16, start, pieces, banks, copies):
-            width = sum(pieces)
+        def finish(z_part, start, widths, banks, copies):
+            width = sum(widths)
             z_codes = keep.tile([P, width], U32, name=f"z_codes{start}", align_bytes=64)
             z_scales = keep.tile([P, width], U8, name=f"z_scales{start}", align_bytes=64)
             result = keep.tile([P, N // P, width], F32, name=f"result{start}")
             accs = [bank(b) for b in banks]
             lo = 0
-            for piece in pieces:
+            for piece in widths:
                 cols = slice(lo, lo + piece)
-                quantize(z_codes[:, cols], z_scales[:, cols], z16[:, cols, :].rearrange("p v t -> p (v t)"))
+                quantize(z_codes[:, cols], z_scales[:, cols], z_part[:, cols, :].rearrange("p v t -> p (v t)"))
                 for g in range(N // P):
                     nc.tensor.matmul_mx(
                         out=accs[g][:, cols],
@@ -248,16 +269,15 @@ def tile_picked_wedgecv_relu_l_kernel(
                 copies[g](out=result[:, g, :], in_=accs[g][:, :width])
             nc.sync.dma_start(out=out_view[:, :, start : start + width], in_=result[:])
 
-        tail_edge = []
-        for d, (start, width), pieces, banks in zip(range(2), PARTS, ((512,), (256, 128)), ((6, 7), (2, 3))):
-            z16 = keep.tile([P, width, PACK], BF16, name=f"z16_{start}", tag=f"z{d}", align_bytes=64)
-            nc.vector.tensor_tensor(z16[:], rounded[0, start][:], rounded[1, start][:], MAX)
-            finish(z16, start, pieces, banks, (nc.scalar.copy, nc.scalar.copy))
-            tail_edge.append(keep.tile([P, PACK, TAIL], F32, name=f"tail_edge{d}", tag=f"z{d}", align_bytes=64))
-            for t in range(PACK):
-                edge(tail_edge[d][:, t, :], d, t, MAIN, TAIL, y_tail[:, t, :])
-            if d == 0:
-                tail_rounded = round_edges(tail_edge[0][:], "tail_rounded")
-        z16 = keep.tile([P, TAIL, PACK], BF16, name="z16_tail", align_bytes=64)
-        nc.vector.tensor_tensor(woven(z16[:]), woven(tail_rounded[:]), planar(tail_edge[1][:]), MAX)
-        finish(z16, MAIN, (TAIL,), (4, 5), (nc.scalar.copy, nc.vector.tensor_copy))
+        tail_edges1 = keep.tile([P, PACK, TAIL], F32, name="tail_edges1", tag=f"rounded0_{BANK}", align_bytes=64)
+        for t in range(PACK):
+            edge(tail_edges1[:, t, :], 0, t, MAIN, TAIL, y_tail[:, t, :])
+        tail_woven1 = relu_and_weave(tail_edges1[:], "tail_woven1")
+        for z_part, start, widths, banks in zip(z_woven, (0, BANK), ((BANK,), (WIDE, NARROW)), ((6, 7), (2, 3))):
+            finish(z_part, start, widths, banks, (nc.scalar.copy, nc.scalar.copy))
+        tail_edges2 = keep.tile([P, PACK, TAIL], F32, name="tail_edges2", tag=f"z_woven{BANK}", align_bytes=64)
+        for t in range(PACK):
+            edge(tail_edges2[:, t, :], 1, t, MAIN, TAIL, y_tail[:, t, :])
+        z_tail = keep.tile([P, TAIL, PACK], BF16, name="z_tail", align_bytes=64)
+        nc.vector.tensor_tensor(woven(z_tail[:]), woven(tail_woven1[:]), planar(tail_edges2[:]), MAX)
+        finish(z_tail, MAIN, (TAIL,), (0, 5), (nc.scalar.copy, nc.vector.tensor_copy))

from contextlib import ExitStack

import concourse.mybir as mybir

K, T, H, N = 512, 1024, 512, 256
FLOPS = 2 * K * H * T * 2 + 2 * H * N * T

F32 = mybir.dt.float32
BF16 = mybir.dt.bfloat16
I32 = mybir.dt.int32
U32 = mybir.dt.uint32
U16 = mybir.dt.uint16
U8 = mybir.dt.uint8
FP8X4 = mybir.dt.float8_e4m3fn_x4
ADD = mybir.AluOpType.add
MAX = mybir.AluOpType.max
RELU = mybir.ActivationFunctionType.Relu

P = 128
PACK = 4
BANK = 512
STRIPE = 16
RUN = 4
W_PIECES = ((0, 320), (320, 192))
E0_PIECES = ((0, 256), (256, 256), (512, 256), (768, 128), (896, 128))
E0_BANKS = (0, 1, 2, 4, 3)
MAIN = 896
TAIL = T - MAIN
PARTS = ((0, BANK), (BANK, MAIN - BANK))
WIDE, NARROW = 256, 128


def tile_picked_wedgecv_relu_l_kernel(
    tc, x_words, x_scales, w1, w2, w3, pos1, pos2, out
):
    nc = tc.nc
    with ExitStack() as ctx:
        keep = ctx.enter_context(tc.tile_pool(name="keep", bufs=1))
        psum = ctx.enter_context(tc.psum_pool(name="psum", bufs=1))

        def bank(b):
            return psum.tile([P, BANK], F32, name=f"bank{b}")

        list1 = keep.tile([P, T // STRIPE], U16, name="list1")
        list2 = keep.tile([P, T // STRIPE], U16, name="list2")

        x_scale_rows = keep.tile([P, T], U8, name="x_scale_rows", align_bytes=64)
        nc.vector.memset(x_scale_rows[:].bitcast(U32), 0)
        for q in range(4):
            nc.sync.dma_start(
                out=x_scale_rows[32 * q : 32 * q + 4, :].bitcast(I32),
                in_=x_scales[0, 4 * q : 4 * q + 4, :].bitcast(I32),
            )

        def load_pieces(w, name):
            pieces = []
            for first, width in W_PIECES:
                raw = keep.tile(
                    [P, PACK, width], F32, name=f"{name}_raw{first}", tag=f"{name}_raw{first}", align_bytes=64
                )
                nc.sync.dma_start(out=raw[:], in_=w[:, first : first + width].rearrange("(p j) c -> p j c", j=PACK))
                pieces.append(raw)
            return pieces

        w2_raw = load_pieces(w2, "w2")
        x_bytes = x_words[0].rearrange("p n r -> p (n r)")
        x_codes = []
        for h in range(T // BANK):
            codes = keep.tile([P, BANK], U32, name=f"x_codes{h}", align_bytes=64)
            nc.sync.dma_start(
                out=codes[:].bitcast(I32),
                in_=x_bytes[:, h * BANK * PACK : (h + 1) * BANK * PACK].bitcast(I32),
            )
            x_codes.append(codes)
        nc.sync.dma_start(list1[:], pos1)
        nc.sync.dma_start(list2[:], pos2)
        w1_raw = load_pieces(w1, "w1")
        w3_raw = keep.tile([P, PACK, N], F32, name="w3_raw")
        nc.sync.dma_start(out=w3_raw[:], in_=w3.rearrange("(p j) c -> p j c", j=PACK))

        def deal_columns(copy, raw, first, m_lo, m_hi, grouped):
            m0 = first // PACK
            copy(
                out=grouped[:, :, m0 + m_lo : m0 + m_hi, :].rearrange("p t m j -> p m j t"),
                in_=raw[:, :, m_lo * PACK : m_hi * PACK].rearrange("p j (m t) -> p m j t", t=PACK),
            )

        def quantize(codes, scales, values):
            nc.vector.quantize_mx(out=codes.bitcast(FP8X4), scales=scales, in_=values)

        def project(acc, w_codes, w_scales, t, start, width):
            h, lo = divmod(start, BANK)
            rows = slice(t * P, (t + 1) * P)
            nc.tensor.matmul_mx(
                out=acc,
                lhsT=w_codes[:, rows].bitcast(FP8X4),
                lhsT_scale=w_scales[:, rows],
                rhs=x_codes[h][:, lo : lo + width].bitcast(FP8X4),
                rhs_scale=x_scale_rows[:, start : start + width],
                start=True,
                stop=True,
            )

        w2_grouped = keep.tile([P, PACK, P, PACK], BF16, name="w2_grouped", align_bytes=64)
        w2_codes = keep.tile([P, H], U32, name="w2_codes", align_bytes=64)
        w2_scales = keep.tile([P, H], U8, name="w2_scales", align_bytes=64)
        for (first, width), raw in zip(W_PIECES, w2_raw):
            groups = width // PACK
            vector_groups = groups // 3 * 2
            deal_columns(nc.vector.tensor_copy, raw, first, 0, vector_groups, w2_grouped)
            deal_columns(nc.scalar.copy, raw, first, vector_groups, groups, w2_grouped)
        w2_flat = w2_grouped[:].rearrange("p t m j -> p (t m j)")
        for lo, hi in ((0, P), (P, 2 * P), (2 * P, H)):
            quantize(w2_codes[:, lo:hi], w2_scales[:, lo:hi], w2_flat[:, lo * PACK : hi * PACK])

        e_rows = {0: keep.tile([P, T], F32, name="e_rows0")}

        def make_e(t, tag):
            e_rows[t] = keep.tile([P, T], F32, name=f"e_rows{t}", tag=tag, align_bytes=64)
            for h in range(T // BANK):
                acc = bank(2 + h)
                project(acc[:], w2_codes, w2_scales, t, h * BANK, BANK)
                nc.scalar.copy(out=e_rows[t][:, h * BANK : (h + 1) * BANK], in_=acc[:])

        for q, (start, width) in enumerate(E0_PIECES):
            acc = bank(E0_BANKS[q])
            project(acc[:, :width], w2_codes, w2_scales, 0, start, width)
            copy = nc.vector.tensor_copy if q % 2 else nc.scalar.copy
            copy(out=e_rows[0][:, start : start + width], in_=acc[:, :width])

        lists = (list1, list2)

        def neighbours(d, t, start, width):
            return e_rows[t][:].indirect(lists[d][:, start // STRIPE : (start + width) // STRIPE])

        def pick(d, start, width, name, tag):
            picked = keep.tile([P, width], F32, name=name, tag=tag, align_bytes=64)
            nc.vector.tensor_copy(picked[:], neighbours(d, 0, start, width))
            return picked

        pick1 = pick(0, 0, MAIN, "pick1", "pick1")
        pick2_low = pick(1, 0, BANK, "pick2_low", "pick2_low_then_w3")

        w1_grouped = keep.tile([P, PACK, P, PACK], BF16, name="w1_grouped", tag="w1_then_pick2_high", align_bytes=64)
        w1_codes = keep.tile([P, H], U32, name="w1_codes", align_bytes=64)
        w1_scales = keep.tile([P, H], U8, name="w1_scales", align_bytes=64)
        for (first, width), raw in zip(W_PIECES, w1_raw):
            deal_columns(nc.scalar.copy, raw, first, 0, width // PACK, w1_grouped)
        make_e(1, f"w1_raw{W_PIECES[-1][0]}")
        quantize(w1_codes[:], w1_scales[:], w1_grouped[:].rearrange("p t m j -> p (t m j)"))
        pick2_high = pick(1, BANK, MAIN - BANK, "pick2_high", "w1_then_pick2_high")

        def centre(acc, lo, t, start, width):
            project(acc[:, lo : lo + width], w1_codes, w1_scales, t, start, width)

        mid_edges = [keep.tile([P, 2, MAIN], F32, name=f"mid_edges{d}") for d in range(2)]
        z_planar = keep.tile([P, PACK, MAIN], BF16, name="z_planar")
        larger_e0 = keep.tile([P, MAIN], F32, name="larger_e0")
        nc.vector.tensor_tensor(larger_e0[:, :BANK], pick1[:, :BANK], pick2_low[:], MAX)
        nc.vector.tensor_tensor(larger_e0[:, BANK:], pick1[:, BANK:], pick2_high[:], MAX)
        y1 = keep.tile([P, MAIN], F32, name="y1", align_bytes=64)
        y23 = keep.tile([P, 2, MAIN], F32, name="y23", align_bytes=64)
        y_tail = keep.tile([P, PACK, TAIL], F32, name="y_tail")

        y0_low = bank(1)
        centre(y0_low, 0, 0, 0, BANK)
        acc = bank(0)
        centre(acc, 0, 1, 0, BANK)
        nc.scalar.copy(out=y1[:, :BANK], in_=acc[:])
        acc = bank(4)
        centre(acc, 0, 1, BANK, WIDE)
        centre(acc, WIDE, 1, BANK + WIDE, NARROW)
        nc.scalar.copy(out=y1[:, BANK:], in_=acc[:, : MAIN - BANK])
        y0_high = bank(5)
        centre(y0_high, 0, 0, BANK, WIDE)
        centre(y0_high, WIDE, 0, BANK + WIDE, NARROW)
        nc.vector.tensor_tensor(z_planar[:, 0, :BANK], larger_e0[:, :BANK], y0_low[:], ADD)
        nc.vector.tensor_tensor(z_planar[:, 0, BANK:], larger_e0[:, BANK:], y0_high[:, : MAIN - BANK], ADD)

        def edge(dst, d, t, start, width, y):
            nc.vector.tensor_tensor(dst, neighbours(d, t, start, width), y, ADD)

        for d in range(2):
            edge(mid_edges[d][:, 0, :], d, 1, 0, MAIN, y1[:])

        make_e(2, "e_rows2")
        make_e(3, "e_rows3")
        for i in range(2):
            acc = bank(6 + i)
            centre(acc, 0, 2 + i, 0, BANK)
            nc.scalar.copy(out=y23[:, i, :BANK], in_=acc[:])
        for b, start, width in ((0, BANK + WIDE, NARROW), (4, BANK, WIDE)):
            acc = bank(b)
            for i in range(2):
                centre(acc, i * width, 2 + i, start, width)
            nc.scalar.copy(
                out=y23[:, :, start : start + width],
                in_=acc[:, : 2 * width].rearrange("p (i v) -> p i v", i=2),
            )

        w3_grouped = keep.tile([P, N, PACK], BF16, name="w3_grouped", tag="pick2_low_then_w3", align_bytes=64)
        w3_codes = keep.tile([P, N], U32, name="w3_codes", align_bytes=64)
        w3_scales = keep.tile([P, N], U8, name="w3_scales", align_bytes=64)
        nc.scalar.copy(
            out=w3_grouped[:].rearrange("p (c i) j -> p c j i", i=RUN),
            in_=w3_raw[:].rearrange("p j (c i) -> p c j i", i=RUN),
        )
        acc = bank(4)
        for t in range(PACK):
            centre(acc, t * TAIL, t, MAIN, TAIL)
        nc.scalar.copy(out=y_tail[:].rearrange("p t v -> p (t v)"), in_=acc[:])

        def woven(ap):
            return ap.rearrange("p (c i) t -> p c t i", i=RUN)

        def planar(ap):
            return ap.rearrange("p t (c i) -> p c t i", i=RUN)

        def relu_and_weave(src, name):
            dst = keep.tile([P, src.shape[2], PACK], BF16, name=name, tag=name, align_bytes=64)
            nc.scalar.activation(out=woven(dst[:]), in_=planar(src), func=RELU)
            return dst

        for d in range(2):
            edge(mid_edges[d][:, 1, :], d, 2, 0, MAIN, y23[:, 0, :])
        quantize(w3_codes[:], w3_scales[:], w3_grouped[:].rearrange("p n j -> p (n j)"))
        rounded = {}
        for d in range(2):
            for start, width in PARTS:
                rounded[d, start] = keep.tile(
                    [P, 2, width], BF16, name=f"rounded{d}_{start}", tag=f"rounded{d}_{start}", align_bytes=64
                )
                nc.scalar.copy(out=rounded[d, start][:], in_=mid_edges[d][:, :, start : start + width])
        last_edge1 = keep.tile([P, MAIN], F32, name="last_edge1")
        edge(last_edge1[:], 0, 3, 0, MAIN, y23[:, 1, :])
        z_woven = []
        for (start, width), tag in zip(PARTS, ("last_edge2_0", "rounded0_0")):
            cols = slice(start, start + width)
            last_edge2 = keep.tile([P, width], F32, name=f"last_edge2_{start}", tag=tag, align_bytes=64)
            edge(last_edge2[:], 1, 3, start, width, y23[:, 1, cols])
            nc.vector.tensor_tensor(z_planar[:, 1:3, cols], rounded[0, start][:], rounded[1, start][:], MAX)
            nc.vector.tensor_tensor(z_planar[:, 3, cols], last_edge1[:, cols], last_edge2[:], MAX)
            z_woven.append(relu_and_weave(z_planar[:, :, cols], f"z_woven{start}"))

        out_view = out.rearrange("(g p) v -> p g v", p=P)

        def finish(z_part, start, widths, banks, copies):
            width = sum(widths)
            z_codes = keep.tile([P, width], U32, name=f"z_codes{start}", align_bytes=64)
            z_scales = keep.tile([P, width], U8, name=f"z_scales{start}", align_bytes=64)
            result = keep.tile([P, N // P, width], F32, name=f"result{start}")
            accs = [bank(b) for b in banks]
            lo = 0
            for piece in widths:
                cols = slice(lo, lo + piece)
                quantize(z_codes[:, cols], z_scales[:, cols], z_part[:, cols, :].rearrange("p v t -> p (v t)"))
                for g in range(N // P):
                    nc.tensor.matmul_mx(
                        out=accs[g][:, cols],
                        lhsT=w3_codes[:, g * P : (g + 1) * P].bitcast(FP8X4),
                        lhsT_scale=w3_scales[:, g * P : (g + 1) * P],
                        rhs=z_codes[:, cols].bitcast(FP8X4),
                        rhs_scale=z_scales[:, cols],
                        start=True,
                        stop=True,
                    )
                lo += piece
            for g in range(N // P):
                copies[g](out=result[:, g, :], in_=accs[g][:, :width])
            nc.sync.dma_start(out=out_view[:, :, start : start + width], in_=result[:])

        tail_edges1 = keep.tile([P, PACK, TAIL], F32, name="tail_edges1", tag=f"rounded0_{BANK}", align_bytes=64)
        for t in range(PACK):
            edge(tail_edges1[:, t, :], 0, t, MAIN, TAIL, y_tail[:, t, :])
        tail_woven1 = relu_and_weave(tail_edges1[:], "tail_woven1")
        for z_part, start, widths, banks in zip(z_woven, (0, BANK), ((BANK,), (WIDE, NARROW)), ((6, 7), (2, 3))):
            finish(z_part, start, widths, banks, (nc.scalar.copy, nc.scalar.copy))
        tail_edges2 = keep.tile([P, PACK, TAIL], F32, name="tail_edges2", tag=f"z_woven{BANK}", align_bytes=64)
        for t in range(PACK):
            edge(tail_edges2[:, t, :], 1, t, MAIN, TAIL, y_tail[:, t, :])
        z_tail = keep.tile([P, TAIL, PACK], BF16, name="z_tail", align_bytes=64)
        nc.vector.tensor_tensor(woven(z_tail[:]), woven(tail_woven1[:]), planar(tail_edges2[:]), MAX)
        finish(z_tail, MAIN, (TAIL,), (0, 5), (nc.scalar.copy, nc.vector.tensor_copy))
